import numpy as np, ml_dtypes
CORES = [88,89,90,91,92,93,94,95,160,161,162,163,164,165,166,167]
N = 16
def setup_inputs(rng):
    return {"x": rng.standard_normal((N, 128, 2048), dtype=np.float32).astype(ml_dtypes.bfloat16)}
def reference(x):
    s = x.sum(axis=0, dtype=np.float64).astype(x.dtype)
    return {"y": np.broadcast_to(s, (N,) + s.shape)}

@@ -1,0 +1,151 @@
+from concourse.bass import DstId, RemoteDMATransfer
+from concourse.mybir import AluOpType
+
+
+def _plan_direct(nw):
+    gx = {0: 2, 3: 2, 1: 3, 2: 3, 4: 6, 7: 6, 5: 7, 6: 7}
+    return [(16 // nw, [(h, gx[h], False) for h in range(8)]) for _ in range(nw)]
+
+
+def _plan_two_ways(rows_b):
+    return [(rows_b, [(o, o ^ 1, True) for o in (0, 1, 4, 5)]),
+            (32 - rows_b, [(o, o ^ 1, False) for o in (2, 3, 6, 7)])]
+
+
+WAVES = _plan_direct(2)
+STORE_BY_WAVE = False
+
+SCRATCH = {}
+SEMAPHORES = ["sent", "acc", "st"]
+ROW0 = []
+_r = 0
+for _q, (_nr, _ps) in enumerate(WAVES):
+    _w = 16 * _nr
+    _k = max(sum(1 for _p in _ps if _p[1] == _g) for _g in range(8))
+    SCRATCH["xs%d" % _q] = ("dram", [len(_ps), 128, _w], "bfloat16")
+    SCRATCH["land%d" % _q] = ("dram", [7 * _k, 128, _w], "bfloat16")
+    SCRATCH["sa%d" % _q] = ("dram", [128, _w], "bfloat16")
+    SCRATCH["sb%d" % _q] = ("dram", [128, _w], "bfloat16")
+    SCRATCH["out%d" % _q] = ("dram", [len(_ps), 128, _w], "bfloat16")
+    if any(_p[2] for _p in _ps):
+        SCRATCH["rl%d" % _q] = ("dram", [128, _w], "bfloat16")
+        SEMAPHORES.append("rl%d" % _q)
+    SEMAPHORES += [_n + "%d" % _q for _n in ("ld", "arr", "pa", "pb", "fin", "sta")]
+    ROW0.append(_r)
+    _r += _nr * len(_ps)
+
+
+def rank_program(g, core, T, topo):
+    S = T.sem
+    bases = sorted({k - k % 8 for k in T.cores})
+    c = core % 8
+    base = core - c
+
+    def dst(d):
+        rid, pid = topo.addr(d, core)
+        return DstId(rid=rid, pnc=pid)
+
+    if T.rank_of(core) is None:
+        if (base ^ 8) in bases:
+            for q, (nr, ps) in enumerate(WAVES):
+                for (o, gc, rel) in ps:
+                    if rel and o + 2 == c:
+                        rid, pid = topo.addr((base ^ 8) + o, core)
+                        g.wait_ge(S["rl%d" % q], 8)
+                        g.remote_dma(out_ap=T["sb%d" % q][:], in_ap=T["rl%d" % q][:], remote_sem=S["pb%d" % q],
+                                     local_sem=S.sent, pid=pid, routing_id=rid, dma_engine_mask=0xFF)
+                        g.wait_ge(S.sent, 8)
+        return
+
+    peer = [b for b in bases if b != base][0]
+    nsent = 0
+    nst = 0
+    nacc = 0
+
+    for q, (nr, ps) in enumerate(WAVES):
+        eng = g.sync if q % 2 == 0 else g.scalar
+        eng.dma_start(T["xs%d" % q][:], T.x[ROW0[q]:ROW0[q] + nr * len(ps), :]).then_inc(S["ld%d" % q], 16)
+
+    for q, (nr, ps) in enumerate(WAVES):
+        g.wait_ge(S["ld%d" % q], 16)
+        es = 16 // len(ps)
+        tr = []
+        for i, (o, gc, rel) in enumerate(ps):
+            if gc == c:
+                continue
+            k = [j for j, p in enumerate(ps) if p[1] == gc].index(i)
+            slot = 7 * k + (c if c < gc else c - 1)
+            tr.append(RemoteDMATransfer(dst_ids=[dst(base + gc)], dma_engine_mask=((1 << es) - 1) << (es * len(tr)),
+                                        remote_sem=S["arr%d" % q], srcs=[T["xs%d" % q][i]],
+                                        dsts=[T["land%d" % q][slot]], alu_op=0))
+        g.remote_dma_fused(tr, local_sem=S.sent)
+        nsent += es * len(tr)
+
+    for q, (nr, ps) in enumerate(WAVES):
+        mine = [i for i, p in enumerate(ps) if p[1] == c]
+        if not mine:
+            continue
+        g.wait_ge(S["arr%d" % q], 7 * len(mine) * (16 // len(ps)))
+        ef = 8 // len(mine)
+        tr = []
+        for k, i in enumerate(mine):
+            o, gc, rel = ps[i]
+            srcs = [T["land%d" % q][7 * k + j] for j in range(7)] + [T["xs%d" % q][i]]
+            m = ((1 << ef) - 1) << (ef * k)
+            if rel:
+                far, fbuf, fsem = (peer ^ 8) + o + 2, T["rl%d" % q][:], S["rl%d" % q]
+            else:
+                far, fbuf, fsem = peer + o, T["sb%d" % q][:], S["pb%d" % q]
+            tr.append(RemoteDMATransfer(dst_ids=[dst(far)], dma_engine_mask=m, remote_sem=fsem,
+                                        srcs=srcs, dsts=[fbuf], alu_op=1))
+            tr.append(RemoteDMATransfer(dst_ids=[dst(base + o)], dma_engine_mask=m << 8, remote_sem=S["pa%d" % q],
+                                        srcs=srcs, dsts=[T["sa%d" % q][:]], alu_op=1))
+        g.remote_dma_fused(tr, local_sem=S.sent)
+        nsent += 2 * ef * len(mine)
+
+    own = []
+    for q, (nr, ps) in enumerate(WAVES):
+        for i, (o, gc, rel) in enumerate(ps):
+            if o != c:
+                continue
+            ef = 8 // sum(1 for p in ps if p[1] == gc)
+            r0 = ROW0[q] + nr * i
+            own.append((q, r0, nr))
+            g.sync.wait_ge(S["pa%d" % q], ef)
+            g.sync.dma_start(T.y[r0:r0 + nr, :], T["sa%d" % q][:]).then_inc(S["sta%d" % q], 16)
+            g.wait_ge(S["pa%d" % q], ef)
+            g.wait_ge(S["pb%d" % q], 8 if rel else ef)
+            others = [d for d in range(8) if d != c]
+            g.remote_dma_fused([RemoteDMATransfer(dst_ids=[dst(base + d) for d in others], dma_engine_mask=0xFFFF,
+                                                  remote_sem=S["fin%d" % q],
+                                                  srcs=[T["sa%d" % q][:], T["sb%d" % q][:]],
+                                                  dsts=[T["out%d" % q][i] for d in others], alu_op=1)],
+                               local_sem=S.sent)
+            nsent += 16
+
+    for (q, r0, nr) in own:
+        g.wait_ge(S["sta%d" % q], 16)
+        g.dma_start(T.y[r0:r0 + nr, :], T["sb%d" % q][:], accum_op=AluOpType.add,
+                    max_dma_last_dim=4096).then_inc(S.acc, 16)
+        nacc += 16
+
+    for q, (nr, ps) in enumerate(WAVES):
+        nf = 16 * sum(1 for p in ps if p[0] != c)
+        mine = [i for i, p in enumerate(ps) if p[0] == c]
+        runs = [(0, len(ps))] if not mine else [(0, mine[0]), (mine[0] + 1, len(ps))]
+        for j, (a, b) in enumerate(runs):
+            if a == b:
+                continue
+            if STORE_BY_WAVE:
+                eng = g.sync if mine else g.scalar
+            else:
+                eng = g.sync if j == 0 else g.scalar
+            eng.wait_ge(S["fin%d" % q], nf)
+            eng.dma_start(T.y[ROW0[q] + nr * a:ROW0[q] + nr * b, :], T["out%d" % q][a:b]).then_inc(S.st, 16)
+            nst += 16
+
+    for q, (nr, ps) in enumerate(WAVES):
+        g.wait_ge(S["fin%d" % q], 16 * sum(1 for p in ps if p[0] != c))
+    g.wait_ge(S.st, nst)
+    g.wait_ge(S.acc, nacc)
+    g.wait_ge(S.sent, nsent)

@@ -2,18 +2,12 @@ from concourse.bass import DstId, RemoteDMATransfer
 from concourse.mybir import AluOpType
 
 
-def _plan_direct(nw):
-    gx = {0: 2, 3: 2, 1: 3, 2: 3, 4: 6, 7: 6, 5: 7, 6: 7}
-    return [(16 // nw, [(h, gx[h], False) for h in range(8)]) for _ in range(nw)]
-
-
 def _plan_two_ways(rows_b):
     return [(rows_b, [(o, o ^ 1, True) for o in (0, 1, 4, 5)]),
             (32 - rows_b, [(o, o ^ 1, False) for o in (2, 3, 6, 7)])]
 
 
-WAVES = _plan_direct(2)
-STORE_BY_WAVE = False
+WAVES = _plan_two_ways(16)
 
 SCRATCH = {}
 SEMAPHORES = ["sent", "acc", "st"]
@@ -133,13 +127,10 @@ def rank_program(g, core, T, topo):
         nf = 16 * sum(1 for p in ps if p[0] != c)
         mine = [i for i, p in enumerate(ps) if p[0] == c]
         runs = [(0, len(ps))] if not mine else [(0, mine[0]), (mine[0] + 1, len(ps))]
-        for j, (a, b) in enumerate(runs):
+        for (a, b) in runs:
             if a == b:
                 continue
-            if STORE_BY_WAVE:
-                eng = g.sync if mine else g.scalar
-            else:
-                eng = g.sync if j == 0 else g.scalar
+            eng = g.sync if mine else g.scalar
             eng.wait_ge(S["fin%d" % q], nf)
             eng.dma_start(T.y[ROW0[q] + nr * a:ROW0[q] + nr * b, :], T["out%d" % q][a:b]).then_inc(S.st, 16)
             nst += 16

@@ -2,12 +2,15 @@ from concourse.bass import DstId, RemoteDMATransfer
 from concourse.mybir import AluOpType
 
 
-def _plan_two_ways(rows_b):
-    return [(rows_b, [(o, o ^ 1, True) for o in (0, 1, 4, 5)]),
-            (32 - rows_b, [(o, o ^ 1, False) for o in (2, 3, 6, 7)])]
+def _plan_two_ways(shares):
+    plan = []
+    for (rows_b, rows_a) in shares:
+        plan.append((rows_b, [(o, o ^ 1, True) for o in (0, 1, 4, 5)]))
+        plan.append((rows_a, [(o, o ^ 1, False) for o in (2, 3, 6, 7)]))
+    return plan
 
 
-WAVES = _plan_two_ways(16)
+WAVES = _plan_two_ways([(8, 8), (8, 8)])
 
 SCRATCH = {}
 SEMAPHORES = ["sent", "acc", "st"]
@@ -41,6 +44,7 @@ def rank_program(g, core, T, topo):
 
     if T.rank_of(core) is None:
         if (base ^ 8) in bases:
+            n = 0
             for q, (nr, ps) in enumerate(WAVES):
                 for (o, gc, rel) in ps:
                     if rel and o + 2 == c:
@@ -48,7 +52,9 @@ def rank_program(g, core, T, topo):
                         g.wait_ge(S["rl%d" % q], 8)
                         g.remote_dma(out_ap=T["sb%d" % q][:], in_ap=T["rl%d" % q][:], remote_sem=S["pb%d" % q],
                                      local_sem=S.sent, pid=pid, routing_id=rid, dma_engine_mask=0xFF)
-                        g.wait_ge(S.sent, 8)
+                        n += 8
+            if n:
+                g.wait_ge(S.sent, n)
         return
 
     peer = [b for b in bases if b != base][0]

from concourse.bass import DstId, RemoteDMATransfer
from concourse.mybir import AluOpType


def _plan_two_ways(shares):
    plan = []
    for (rows_b, rows_a) in shares:
        plan.append((rows_b, [(o, o ^ 1, True) for o in (0, 1, 4, 5)]))
        plan.append((rows_a, [(o, o ^ 1, False) for o in (2, 3, 6, 7)]))
    return plan


WAVES = _plan_two_ways([(8, 8), (8, 8)])

SCRATCH = {}
SEMAPHORES = ["sent", "acc", "st"]
ROW0 = []
_r = 0
for _q, (_nr, _ps) in enumerate(WAVES):
    _w = 16 * _nr
    _k = max(sum(1 for _p in _ps if _p[1] == _g) for _g in range(8))
    SCRATCH["xs%d" % _q] = ("dram", [len(_ps), 128, _w], "bfloat16")
    SCRATCH["land%d" % _q] = ("dram", [7 * _k, 128, _w], "bfloat16")
    SCRATCH["sa%d" % _q] = ("dram", [128, _w], "bfloat16")
    SCRATCH["sb%d" % _q] = ("dram", [128, _w], "bfloat16")
    SCRATCH["out%d" % _q] = ("dram", [len(_ps), 128, _w], "bfloat16")
    if any(_p[2] for _p in _ps):
        SCRATCH["rl%d" % _q] = ("dram", [128, _w], "bfloat16")
        SEMAPHORES.append("rl%d" % _q)
    SEMAPHORES += [_n + "%d" % _q for _n in ("ld", "arr", "pa", "pb", "fin", "sta")]
    ROW0.append(_r)
    _r += _nr * len(_ps)


def rank_program(g, core, T, topo):
    S = T.sem
    bases = sorted({k - k % 8 for k in T.cores})
    c = core % 8
    base = core - c

    def dst(d):
        rid, pid = topo.addr(d, core)
        return DstId(rid=rid, pnc=pid)

    if T.rank_of(core) is None:
        if (base ^ 8) in bases:
            n = 0
            for q, (nr, ps) in enumerate(WAVES):
                for (o, gc, rel) in ps:
                    if rel and o + 2 == c:
                        rid, pid = topo.addr((base ^ 8) + o, core)
                        g.wait_ge(S["rl%d" % q], 8)
                        g.remote_dma(out_ap=T["sb%d" % q][:], in_ap=T["rl%d" % q][:], remote_sem=S["pb%d" % q],
                                     local_sem=S.sent, pid=pid, routing_id=rid, dma_engine_mask=0xFF)
                        n += 8
            if n:
                g.wait_ge(S.sent, n)
        return

    peer = [b for b in bases if b != base][0]
    nsent = 0
    nst = 0
    nacc = 0

    for q, (nr, ps) in enumerate(WAVES):
        eng = g.sync if q % 2 == 0 else g.scalar
        eng.dma_start(T["xs%d" % q][:], T.x[ROW0[q]:ROW0[q] + nr * len(ps), :]).then_inc(S["ld%d" % q], 16)

    for q, (nr, ps) in enumerate(WAVES):
        g.wait_ge(S["ld%d" % q], 16)
        es = 16 // len(ps)
        tr = []
        for i, (o, gc, rel) in enumerate(ps):
            if gc == c:
                continue
            k = [j for j, p in enumerate(ps) if p[1] == gc].index(i)
            slot = 7 * k + (c if c < gc else c - 1)
            tr.append(RemoteDMATransfer(dst_ids=[dst(base + gc)], dma_engine_mask=((1 << es) - 1) << (es * len(tr)),
                                        remote_sem=S["arr%d" % q], srcs=[T["xs%d" % q][i]],
                                        dsts=[T["land%d" % q][slot]], alu_op=0))
        g.remote_dma_fused(tr, local_sem=S.sent)
        nsent += es * len(tr)

    for q, (nr, ps) in enumerate(WAVES):
        mine = [i for i, p in enumerate(ps) if p[1] == c]
        if not mine:
            continue
        g.wait_ge(S["arr%d" % q], 7 * len(mine) * (16 // len(ps)))
        ef = 8 // len(mine)
        tr = []
        for k, i in enumerate(mine):
            o, gc, rel = ps[i]
            srcs = [T["land%d" % q][7 * k + j] for j in range(7)] + [T["xs%d" % q][i]]
            m = ((1 << ef) - 1) << (ef * k)
            if rel:
                far, fbuf, fsem = (peer ^ 8) + o + 2, T["rl%d" % q][:], S["rl%d" % q]
            else:
                far, fbuf, fsem = peer + o, T["sb%d" % q][:], S["pb%d" % q]
            tr.append(RemoteDMATransfer(dst_ids=[dst(far)], dma_engine_mask=m, remote_sem=fsem,
                                        srcs=srcs, dsts=[fbuf], alu_op=1))
            tr.append(RemoteDMATransfer(dst_ids=[dst(base + o)], dma_engine_mask=m << 8, remote_sem=S["pa%d" % q],
                                        srcs=srcs, dsts=[T["sa%d" % q][:]], alu_op=1))
        g.remote_dma_fused(tr, local_sem=S.sent)
        nsent += 2 * ef * len(mine)

    own = []
    for q, (nr, ps) in enumerate(WAVES):
        for i, (o, gc, rel) in enumerate(ps):
            if o != c:
                continue
            ef = 8 // sum(1 for p in ps if p[1] == gc)
            r0 = ROW0[q] + nr * i
            own.append((q, r0, nr))
            g.sync.wait_ge(S["pa%d" % q], ef)
            g.sync.dma_start(T.y[r0:r0 + nr, :], T["sa%d" % q][:]).then_inc(S["sta%d" % q], 16)
            g.wait_ge(S["pa%d" % q], ef)
            g.wait_ge(S["pb%d" % q], 8 if rel else ef)
            others = [d for d in range(8) if d != c]
            g.remote_dma_fused([RemoteDMATransfer(dst_ids=[dst(base + d) for d in others], dma_engine_mask=0xFFFF,
                                                  remote_sem=S["fin%d" % q],
                                                  srcs=[T["sa%d" % q][:], T["sb%d" % q][:]],
                                                  dsts=[T["out%d" % q][i] for d in others], alu_op=1)],
                               local_sem=S.sent)
            nsent += 16

    for (q, r0, nr) in own:
        g.wait_ge(S["sta%d" % q], 16)
        g.dma_start(T.y[r0:r0 + nr, :], T["sb%d" % q][:], accum_op=AluOpType.add,
                    max_dma_last_dim=4096).then_inc(S.acc, 16)
        nacc += 16

    for q, (nr, ps) in enumerate(WAVES):
        nf = 16 * sum(1 for p in ps if p[0] != c)
        mine = [i for i, p in enumerate(ps) if p[0] == c]
        runs = [(0, len(ps))] if not mine else [(0, mine[0]), (mine[0] + 1, len(ps))]
        for (a, b) in runs:
            if a == b:
                continue
            eng = g.sync if mine else g.scalar
            eng.wait_ge(S["fin%d" % q], nf)
            eng.dma_start(T.y[ROW0[q] + nr * a:ROW0[q] + nr * b, :], T["out%d" % q][a:b]).then_inc(S.st, 16)
            nst += 16

    for q, (nr, ps) in enumerate(WAVES):
        g.wait_ge(S["fin%d" % q], 16 * sum(1 for p in ps if p[0] != c))
    g.wait_ge(S.st, nst)
    g.wait_ge(S.acc, nacc)
    g.wait_ge(S.sent, nsent)
